import numpy as np
import ml_dtypes


def mxq(x, axis, fmt="e4m3"):
    dtype, down = {"e4m3": (ml_dtypes.float8_e4m3fn, 7), "e5m2": (ml_dtypes.float8_e5m2, 14)}[fmt]
    v = np.moveaxis(np.asarray(x, np.float32).astype(ml_dtypes.bfloat16).astype(np.float64), axis, -1)
    blocks = v.reshape(v.shape[:-1] + (-1, 32))
    amax = np.abs(blocks).max(-1, keepdims=True)
    byte = np.maximum(np.where(amax > 0, np.frexp(amax)[1] - 1 + 127, 0) - down, 1)
    scale = np.exp2(byte - 127.0)
    codes = (blocks / scale).astype(np.float32).astype(dtype).astype(np.float64)
    return np.moveaxis((codes * scale).reshape(v.shape), -1, axis)


WIDE = False


def mx_kscale(k):
    if not WIDE:
        return np.ones(k)
    levels = np.array([10, -10, 5, -5, 0])
    if k % 512:
        return np.exp2(np.random.permutation(np.resize(levels, k // 32))).repeat(32)
    a = np.empty((k // 512, 16))
    for p in range(k // 512):
        a[p, :8] = np.random.permutation(np.resize(levels, 8))
        for g in range(8):
            far = levels[np.abs(levels - a[p, g]) >= 10]
            a[p, g + 8] = far[np.random.randint(len(far))]
    return np.exp2(a.ravel()).repeat(32)


def f64(x):
    return np.asarray(x).astype(np.float64)


def striped(idx):
    return np.tile(np.asarray(idx).reshape(-1, 16).T, (8, 1)).astype(np.uint16)


def unstriped(offs):
    return offs[:16].T.reshape(-1).astype(np.int64)


def striped8(idx):
    return np.asarray(idx).reshape(8, -1, 16).transpose(0, 2, 1).reshape(128, -1).astype(np.uint16)


def unstriped8(offs):
    return offs.reshape(8, 16, -1).transpose(0, 2, 1).reshape(8, -1).astype(np.int64)


def pick8(x, idx, run):
    r = np.arange(len(x))
    return x[r[:, None], idx[r % (8 * run) // run]]


E2M1 = np.array([0.0, 0.5, 1.0, 1.5, 2.0, 3.0, 4.0, 6.0, -0.0, -0.5, -1.0, -1.5, -2.0, -3.0, -4.0, -6.0])


def pack_weight(w, fmt):
    k, n = w.shape
    w = f64(np.asarray(w, np.float32).astype(ml_dtypes.bfloat16)).reshape(k // 32, 32, n)
    amax = np.abs(w).max(1)
    if fmt == "e4m3":
        byte = np.frexp(amax)[1] - 1 + 127 - 7
    else:
        mant, ex = np.frexp(amax / 6.0)
        byte = np.where(mant > 0.5, ex, ex - 1) + 127
    byte = np.clip(np.where(amax > 0, byte, 1), 1, 254)
    scaled = (w * np.exp2(127.0 - byte)[:, None, :]).reshape(k, n).astype(np.float32)
    by_word = np.ascontiguousarray(scaled.reshape(k // 512, 128, 4, n).transpose(0, 1, 3, 2))
    if fmt == "e4m3":
        words = by_word.astype(ml_dtypes.float8_e4m3fn).view(np.uint8)
    else:
        c = by_word.astype(ml_dtypes.float4_e2m1fn).view(np.uint8) & 0xF
        words = (c[..., 0::2] | (c[..., 1::2] << 4)).reshape(k // 512, 128, 2 * n)
    return np.ascontiguousarray(words), np.ascontiguousarray(byte.astype(np.uint8).reshape(k // 512, 16, n))


def unpack_weight(words, scales, fmt):
    g, _, n = scales.shape
    words = np.ascontiguousarray(words).reshape(g, 128, n, -1)
    if fmt == "e4m3":
        vals = words.view(ml_dtypes.float8_e4m3fn).astype(np.float64)
    else:
        nib = np.empty((g, 128, n, 4), np.uint8)
        nib[..., 0::2] = words & 0xF
        nib[..., 1::2] = words >> 4
        vals = E2M1[nib]
    vals = vals * np.repeat(np.exp2(scales.astype(np.float64) - 127.0), 8, axis=1)[..., None]
    return vals.transpose(0, 1, 3, 2).reshape(g * 512, n)


K, J, R, T, F, G, O, C, N, S = 512, 256, 512, 1024, 1024, 384, 128, 512, 256, 1024


def setup_inputs():
    n = np.random.standard_normal
    idx = np.random.permutation(T)[:J]
    idx2 = np.stack([np.random.permutation(F)[:G] for _ in range(8)])
    idx3 = np.stack([np.random.permutation(R)[:G] for _ in range(8)])
    idx4 = np.stack([np.random.permutation(C)[:J] for _ in range(8)])
    idx5 = np.stack([np.random.permutation(C)[:O] for _ in range(8)])
    idx6 = np.stack([np.random.permutation(C)[:O] for _ in range(8)])
    idx7 = np.random.permutation(S)[:N]
    fk = mx_kscale(K)
    fr = mx_kscale(R)
    xtp = pack_weight(n((K, T)) * fk[:, None], "e2m1")
    vsp = pack_weight(n((R, S)) * 1 / np.sqrt(R) / fr[:, None], "e2m1")
    return {
        "xt_words": xtp[0],
        "xt_scales": xtp[1],
        "ua": (np.random.randint(-7, 8, (K, F)).astype(np.float64)).astype(np.float32),
        "ha": ((np.random.randint(8, 25, (K, 1)) / 1024.0) / fk[:, None]).astype(np.float32),
        "sa": (np.random.uniform(0.5, 1.6, (R, 1)) * fr[:, None]).astype(np.float32),
        "sb": (np.random.uniform(0.5, 1.6, (R, 1)) * fr[:, None]).astype(np.float32),
        "vs_words": vsp[0],
        "vs_scales": vsp[1],
        "offs": striped(idx),
        "offs2": striped8(idx2),
        "offs3": striped8(idx3),
        "offs4": striped8(idx4),
        "offs5": striped8(idx5),
        "offs6": striped8(idx6),
        "offs7": striped(idx7),
    }


def reference(xt_words, xt_scales, ua, ha, sa, sb, vs_words, vs_scales, offs, offs2, offs3, offs4, offs5, offs6, offs7):
    idx = unstriped(offs)
    idx2 = unstriped8(offs2)
    idx3 = unstriped8(offs3)
    idx4 = unstriped8(offs4)
    idx5 = unstriped8(offs5)
    idx6 = unstriped8(offs6)
    idx7 = unstriped(offs7)
    xtu = unpack_weight(xt_words, xt_scales, "e2m1")
    vsu = unpack_weight(vs_words, vs_scales, "e2m1")
    wcd = pick8(f64(ua), idx2, 64) * f64(ha)
    wc = np.zeros((K, R))
    wc[np.arange(K)[:, None], idx3[np.arange(K) % 512 // 64]] = wcd
    wcq = mxq(wc, 0, "e4m3")
    xtidxg = xtu[:, idx]
    a = wcq.T @ xtidxg
    pw = np.zeros((R, C))
    pw[np.arange(R)[:, None], idx4[np.arange(R) % 512 // 64]] = a
    hid = np.maximum(pick8(pw, idx5, 64) * f64(sa), pick8(pw, idx6, 64) * f64(sb))
    vsidx7g = vsu[:, idx7]
    hidq = mxq(hid, 0, "e4m3")
    y = vsidx7g.T @ hidq
    return y

@@ -1,0 +1,188 @@
+from contextlib import ExitStack
+
+import concourse.mybir as mybir
+
+K, J, R, T, F, G, O, C, N, S = 512, 256, 512, 1024, 1024, 384, 128, 512, 256, 1024
+FLOPS = 2 * K * R * J + 2 * R * N * O
+
+F32 = mybir.dt.float32
+BF16 = mybir.dt.bfloat16
+I32 = mybir.dt.int32
+U32 = mybir.dt.uint32
+U16 = mybir.dt.uint16
+U8 = mybir.dt.uint8
+FP8X4 = mybir.dt.float8_e4m3fn_x4
+FP4X4 = mybir.dt.float4_e2m1fn_x4
+COPY = mybir.ActivationFunctionType.Copy
+MAX = mybir.AluOpType.max
+
+P = 128
+PACK = 4
+
+
+def tile_picked_tokens_sparsecodes_one_boardpair_store_plain_kernel(
+    tc, xt_words, xt_scales, ua, ha, sa, sb, vs_words, vs_scales,
+    offs, offs2, offs3, offs4, offs5, offs6, offs7, out,
+):
+    nc = tc.nc
+    with ExitStack() as ctx:
+        lists = ctx.enter_context(tc.tile_pool(name="lists", bufs=1))
+        keep = ctx.enter_context(tc.tile_pool(name="keep", bufs=1))
+        psum = ctx.enter_context(tc.psum_pool(name="psum", bufs=1))
+
+        def load_list(src, entries, name):
+            tile = lists.tile([P, entries // 16], U16, name=name)
+            nc.sync.dma_start(tile[:], src)
+            return tile
+
+        def load_rowwise(src, name):
+            tile = keep.tile([P, PACK], F32, name=name)
+            nc.sync.dma_start(tile[:], src.rearrange("(p t) one -> p (t one)", t=PACK))
+            return tile
+
+        def load_packed(words, scales, columns, name):
+            word_tile = keep.tile([P, columns], U16, name=name + "_words")
+            nc.sync.dma_start(word_tile[:].bitcast(I32), words[0].bitcast(I32))
+            staged = keep.tile([4, 4, columns // 4], I32, name=name + "_staged")
+            nc.sync.dma_start(staged[:], scales[0].bitcast(I32).rearrange("(q r) c -> r q c", r=4))
+            scale_tile = keep.tile([P, columns], U8, name=name + "_scales")
+            nc.vector.memset(scale_tile[:].bitcast(I32), 0)
+            for q in range(4):
+                nc.vector.tensor_copy(scale_tile[32 * q : 32 * q + 4, :].bitcast(I32), staged[:, q, :])
+            return word_tile, scale_tile
+
+        def gather_packed(word_tile, scale_tile, offsets, entries, name):
+            words = keep.tile([P, entries], U16, name=name + "_words", align_bytes=64)
+            scales = keep.tile([P, entries], U8, name=name + "_scales", align_bytes=64)
+            nc.vector.tensor_copy(words[:], word_tile[:].indirect(offsets[:]))
+            nc.vector.tensor_copy(scales[:], scale_tile[:].indirect(offsets[:]))
+            return words, scales
+
+        wc = [keep.tile([P, R], F32, name=f"wc{t}") for t in range(PACK)]
+        pw = [keep.tile([P, C], F32, name=f"pw{u}") for u in range(PACK)]
+        for tile in wc + pw:
+            nc.vector.memset(tile[:], 0.0)
+
+        ua_rows = ua.rearrange("(p t) f -> p t f", t=PACK)
+        ua_t = [keep.tile([P, F], F32, name=f"ua{t}") for t in range(PACK)]
+
+        def load_plane(t):
+            nc.sync.dma_start(ua_t[t][:], ua_rows[:, t, :])
+
+        load_plane(0)
+        l2 = load_list(offs2, G, "l2")
+        ha_t = load_rowwise(ha, "ha_t")
+        l3 = load_list(offs3, G, "l3")
+        load_plane(1)
+        l1 = load_list(offs, J, "l1")
+        xt_win = load_packed(xt_words, xt_scales, T, "xt")
+        load_plane(2)
+        l7 = load_list(offs7, N, "l7")
+        vs_win = load_packed(vs_words, vs_scales, S, "vs")
+        load_plane(3)
+        l4 = load_list(offs4, J, "l4")
+        l5 = load_list(offs5, O, "l5")
+        l6 = load_list(offs6, O, "l6")
+        sa_t = load_rowwise(sa, "sa_t")
+        sb_t = load_rowwise(sb, "sb_t")
+
+        xg_words, xg_scales = gather_packed(*xt_win, l1, J, "xg")
+        vg_words, vg_scales = gather_packed(*vs_win, l7, N, "vg")
+
+        wcd = [keep.tile([P, G], F32, name=f"wcd{t}") for t in range(PACK)]
+        wc_bf = [keep.tile([P, P, PACK], BF16, name=f"wc_bf{u}", align_bytes=64) for u in range(PACK)]
+
+        def fetch_codes(t):
+            nc.scalar.activation(wcd[t][:], ua_t[t][:].indirect(l2[:]), COPY, scale=ha_t[:, t : t + 1])
+
+        def fill_matrix(t):
+            nc.scalar.activation(wc[t][:].indirect(l3[:]), wcd[t][:], COPY)
+
+        def round_plane(t, u):
+            nc.vector.tensor_copy(wc_bf[u][:, :, t], wc[t][:, u::PACK])
+
+        fetch_codes(0)
+        fill_matrix(0)
+        fetch_codes(1)
+        for t in range(1, PACK):
+            if t + 1 < PACK:
+                fetch_codes(t + 1)
+            fill_matrix(t)
+        for t in range(PACK - 1):
+            for u in range(PACK):
+                round_plane(t, u)
+
+        wq_words = [keep.tile([P, P], U32, name=f"wq_words{u}", align_bytes=64) for u in range(PACK)]
+        wq_scales = [keep.tile([P, P], U8, name=f"wq_scales{u}", align_bytes=64) for u in range(PACK)]
+        a_ps = [psum.tile([P, J], F32, name=f"a_ps{u}") for u in range(PACK)]
+        a_sb = [keep.tile([P, J], F32, name=f"a_sb{u}") for u in range(PACK)]
+
+        def first_product(u):
+            nc.vector.quantize_mx(
+                out=wq_words[u][:].bitcast(FP8X4),
+                scales=wq_scales[u][:],
+                in_=wc_bf[u][:].rearrange("p m t -> p (m t)"),
+            )
+            nc.tensor.matmul_mx(
+                out=a_ps[u][:],
+                lhsT=wq_words[u][:].bitcast(FP8X4),
+                lhsT_scale=wq_scales[u][:],
+                rhs=xg_words[:].bitcast(FP4X4),
+                rhs_scale=xg_scales[:],
+                start=True,
+                stop=True,
+            )
+
+        round_plane(PACK - 1, 0)
+        for u in range(PACK):
+            if u + 1 < PACK:
+                round_plane(PACK - 1, u + 1)
+            first_product(u)
+        nc.scalar.copy(a_sb[0][:], a_ps[0][:])
+        for u in range(1, PACK):
+            nc.vector.tensor_copy(a_sb[u][:], a_ps[u][:])
+
+        first = [keep.tile([P, O], F32, name=f"first{u}") for u in range(PACK)]
+        second = [keep.tile([P, O], F32, name=f"second{u}") for u in range(PACK)]
+        hid_bf = keep.tile([P, O, PACK], BF16, name="hid_bf", align_bytes=64)
+
+        def fill_board(u):
+            nc.scalar.activation(pw[u][:].indirect(l4[:]), a_sb[u][:], COPY)
+
+        def read_board(u):
+            nc.scalar.activation(first[u][:], pw[u][:].indirect(l5[:]), COPY, scale=sa_t[:, u : u + 1])
+            nc.scalar.activation(second[u][:], pw[u][:].indirect(l6[:]), COPY, scale=sb_t[:, u : u + 1])
+            nc.vector.tensor_tensor(hid_bf[:, :, u], first[u][:], second[u][:], MAX)
+
+        fill_board(0)
+        for u in range(PACK):
+            if u + 1 < PACK:
+                fill_board(u + 1)
+            read_board(u)
+
+        hq_words = keep.tile([P, O], U32, name="hq_words", align_bytes=64)
+        hq_scales = keep.tile([P, O], U8, name="hq_scales", align_bytes=64)
+        nc.vector.quantize_mx(
+            out=hq_words[:].bitcast(FP8X4),
+            scales=hq_scales[:],
+            in_=hid_bf[:].rearrange("p o u -> p (o u)"),
+        )
+        for h in range(N // P):
+            cols = slice(h * P, (h + 1) * P)
+            y_ps = psum.tile([P, O], F32, name=f"y_ps{h}")
+            nc.tensor.matmul_mx(
+                out=y_ps[:],
+                lhsT=vg_words[:, cols].bitcast(FP4X4),
+                lhsT_scale=vg_scales[:, cols],
+                rhs=hq_words[:].bitcast(FP8X4),
+                rhs_scale=hq_scales[:],
+                start=True,
+                stop=True,
+            )
+            y_sb = keep.tile([P, O], F32, name=f"y_sb{h}")
+            if h == 0:
+                nc.vector.tensor_copy(y_sb[:], y_ps[:])
+                nc.sync.dma_start(out[cols, :], y_sb[:])
+            else:
+                nc.scalar.copy(y_sb[:], y_ps[:])
+                nc.scalar.dma_start(out[cols, :], y_sb[:])

@@ -58,6 +58,11 @@ def tile_picked_tokens_sparsecodes_one_boardpair_store_plain_kernel(
             nc.vector.tensor_copy(scales[:], scale_tile[:].indirect(offsets[:]))
             return words, scales
 
+        warm_in = keep.tile([P, 1], F32, name="warm_in")
+        warm_out = keep.tile([P, 1], F32, name="warm_out")
+        nc.gpsimd.memset(warm_in[:], 0.0)
+        nc.scalar.activation(warm_out[:], warm_in[:], COPY)
+
         wc = [keep.tile([P, R], F32, name=f"wc{t}") for t in range(PACK)]
         pw = [keep.tile([P, C], F32, name=f"pw{u}") for u in range(PACK)]
         for tile in wc + pw:

from contextlib import ExitStack

import concourse.mybir as mybir

K, J, R, T, F, G, O, C, N, S = 512, 256, 512, 1024, 1024, 384, 128, 512, 256, 1024
FLOPS = 2 * K * R * J + 2 * R * N * O

F32 = mybir.dt.float32
BF16 = mybir.dt.bfloat16
I32 = mybir.dt.int32
U32 = mybir.dt.uint32
U16 = mybir.dt.uint16
U8 = mybir.dt.uint8
FP8X4 = mybir.dt.float8_e4m3fn_x4
FP4X4 = mybir.dt.float4_e2m1fn_x4
COPY = mybir.ActivationFunctionType.Copy
MAX = mybir.AluOpType.max

P = 128
PACK = 4


def tile_picked_tokens_sparsecodes_one_boardpair_store_plain_kernel(
    tc, xt_words, xt_scales, ua, ha, sa, sb, vs_words, vs_scales,
    offs, offs2, offs3, offs4, offs5, offs6, offs7, out,
):
    nc = tc.nc
    with ExitStack() as ctx:
        lists = ctx.enter_context(tc.tile_pool(name="lists", bufs=1))
        keep = ctx.enter_context(tc.tile_pool(name="keep", bufs=1))
        psum = ctx.enter_context(tc.psum_pool(name="psum", bufs=1))

        def load_list(src, entries, name):
            tile = lists.tile([P, entries // 16], U16, name=name)
            nc.sync.dma_start(tile[:], src)
            return tile

        def load_rowwise(src, name):
            tile = keep.tile([P, PACK], F32, name=name)
            nc.sync.dma_start(tile[:], src.rearrange("(p t) one -> p (t one)", t=PACK))
            return tile

        def load_packed(words, scales, columns, name):
            word_tile = keep.tile([P, columns], U16, name=name + "_words")
            nc.sync.dma_start(word_tile[:].bitcast(I32), words[0].bitcast(I32))
            staged = keep.tile([4, 4, columns // 4], I32, name=name + "_staged")
            nc.sync.dma_start(staged[:], scales[0].bitcast(I32).rearrange("(q r) c -> r q c", r=4))
            scale_tile = keep.tile([P, columns], U8, name=name + "_scales")
            nc.vector.memset(scale_tile[:].bitcast(I32), 0)
            for q in range(4):
                nc.vector.tensor_copy(scale_tile[32 * q : 32 * q + 4, :].bitcast(I32), staged[:, q, :])
            return word_tile, scale_tile

        def gather_packed(word_tile, scale_tile, offsets, entries, name):
            words = keep.tile([P, entries], U16, name=name + "_words", align_bytes=64)
            scales = keep.tile([P, entries], U8, name=name + "_scales", align_bytes=64)
            nc.vector.tensor_copy(words[:], word_tile[:].indirect(offsets[:]))
            nc.vector.tensor_copy(scales[:], scale_tile[:].indirect(offsets[:]))
            return words, scales

        warm_in = keep.tile([P, 1], F32, name="warm_in")
        warm_out = keep.tile([P, 1], F32, name="warm_out")
        nc.gpsimd.memset(warm_in[:], 0.0)
        nc.scalar.activation(warm_out[:], warm_in[:], COPY)

        wc = [keep.tile([P, R], F32, name=f"wc{t}") for t in range(PACK)]
        pw = [keep.tile([P, C], F32, name=f"pw{u}") for u in range(PACK)]
        for tile in wc + pw:
            nc.vector.memset(tile[:], 0.0)

        ua_rows = ua.rearrange("(p t) f -> p t f", t=PACK)
        ua_t = [keep.tile([P, F], F32, name=f"ua{t}") for t in range(PACK)]

        def load_plane(t):
            nc.sync.dma_start(ua_t[t][:], ua_rows[:, t, :])

        load_plane(0)
        l2 = load_list(offs2, G, "l2")
        ha_t = load_rowwise(ha, "ha_t")
        l3 = load_list(offs3, G, "l3")
        load_plane(1)
        l1 = load_list(offs, J, "l1")
        xt_win = load_packed(xt_words, xt_scales, T, "xt")
        load_plane(2)
        l7 = load_list(offs7, N, "l7")
        vs_win = load_packed(vs_words, vs_scales, S, "vs")
        load_plane(3)
        l4 = load_list(offs4, J, "l4")
        l5 = load_list(offs5, O, "l5")
        l6 = load_list(offs6, O, "l6")
        sa_t = load_rowwise(sa, "sa_t")
        sb_t = load_rowwise(sb, "sb_t")

        xg_words, xg_scales = gather_packed(*xt_win, l1, J, "xg")
        vg_words, vg_scales = gather_packed(*vs_win, l7, N, "vg")

        wcd = [keep.tile([P, G], F32, name=f"wcd{t}") for t in range(PACK)]
        wc_bf = [keep.tile([P, P, PACK], BF16, name=f"wc_bf{u}", align_bytes=64) for u in range(PACK)]

        def fetch_codes(t):
            nc.scalar.activation(wcd[t][:], ua_t[t][:].indirect(l2[:]), COPY, scale=ha_t[:, t : t + 1])

        def fill_matrix(t):
            nc.scalar.activation(wc[t][:].indirect(l3[:]), wcd[t][:], COPY)

        def round_plane(t, u):
            nc.vector.tensor_copy(wc_bf[u][:, :, t], wc[t][:, u::PACK])

        fetch_codes(0)
        fill_matrix(0)
        fetch_codes(1)
        for t in range(1, PACK):
            if t + 1 < PACK:
                fetch_codes(t + 1)
            fill_matrix(t)
        for t in range(PACK - 1):
            for u in range(PACK):
                round_plane(t, u)

        wq_words = [keep.tile([P, P], U32, name=f"wq_words{u}", align_bytes=64) for u in range(PACK)]
        wq_scales = [keep.tile([P, P], U8, name=f"wq_scales{u}", align_bytes=64) for u in range(PACK)]
        a_ps = [psum.tile([P, J], F32, name=f"a_ps{u}") for u in range(PACK)]
        a_sb = [keep.tile([P, J], F32, name=f"a_sb{u}") for u in range(PACK)]

        def first_product(u):
            nc.vector.quantize_mx(
                out=wq_words[u][:].bitcast(FP8X4),
                scales=wq_scales[u][:],
                in_=wc_bf[u][:].rearrange("p m t -> p (m t)"),
            )
            nc.tensor.matmul_mx(
                out=a_ps[u][:],
                lhsT=wq_words[u][:].bitcast(FP8X4),
                lhsT_scale=wq_scales[u][:],
                rhs=xg_words[:].bitcast(FP4X4),
                rhs_scale=xg_scales[:],
                start=True,
                stop=True,
            )

        round_plane(PACK - 1, 0)
        for u in range(PACK):
            if u + 1 < PACK:
                round_plane(PACK - 1, u + 1)
            first_product(u)
        nc.scalar.copy(a_sb[0][:], a_ps[0][:])
        for u in range(1, PACK):
            nc.vector.tensor_copy(a_sb[u][:], a_ps[u][:])

        first = [keep.tile([P, O], F32, name=f"first{u}") for u in range(PACK)]
        second = [keep.tile([P, O], F32, name=f"second{u}") for u in range(PACK)]
        hid_bf = keep.tile([P, O, PACK], BF16, name="hid_bf", align_bytes=64)

        def fill_board(u):
            nc.scalar.activation(pw[u][:].indirect(l4[:]), a_sb[u][:], COPY)

        def read_board(u):
            nc.scalar.activation(first[u][:], pw[u][:].indirect(l5[:]), COPY, scale=sa_t[:, u : u + 1])
            nc.scalar.activation(second[u][:], pw[u][:].indirect(l6[:]), COPY, scale=sb_t[:, u : u + 1])
            nc.vector.tensor_tensor(hid_bf[:, :, u], first[u][:], second[u][:], MAX)

        fill_board(0)
        for u in range(PACK):
            if u + 1 < PACK:
                fill_board(u + 1)
            read_board(u)

        hq_words = keep.tile([P, O], U32, name="hq_words", align_bytes=64)
        hq_scales = keep.tile([P, O], U8, name="hq_scales", align_bytes=64)
        nc.vector.quantize_mx(
            out=hq_words[:].bitcast(FP8X4),
            scales=hq_scales[:],
            in_=hid_bf[:].rearrange("p o u -> p (o u)"),
        )
        for h in range(N // P):
            cols = slice(h * P, (h + 1) * P)
            y_ps = psum.tile([P, O], F32, name=f"y_ps{h}")
            nc.tensor.matmul_mx(
                out=y_ps[:],
                lhsT=vg_words[:, cols].bitcast(FP4X4),
                lhsT_scale=vg_scales[:, cols],
                rhs=hq_words[:].bitcast(FP8X4),
                rhs_scale=hq_scales[:],
                start=True,
                stop=True,
            )
            y_sb = keep.tile([P, O], F32, name=f"y_sb{h}")
            if h == 0:
                nc.vector.tensor_copy(y_sb[:], y_ps[:])
                nc.sync.dma_start(out[cols, :], y_sb[:])
            else:
                nc.scalar.copy(y_sb[:], y_ps[:])
                nc.scalar.dma_start(out[cols, :], y_sb[:])
